import numpy as np
import ml_dtypes


def mxq(x, axis, fmt="e4m3"):
    dtype, down = {"e4m3": (ml_dtypes.float8_e4m3fn, 7), "e5m2": (ml_dtypes.float8_e5m2, 14)}[fmt]
    v = np.moveaxis(np.asarray(x, np.float32).astype(ml_dtypes.bfloat16).astype(np.float64), axis, -1)
    blocks = v.reshape(v.shape[:-1] + (-1, 32))
    amax = np.abs(blocks).max(-1, keepdims=True)
    byte = np.maximum(np.where(amax > 0, np.frexp(amax)[1] - 1 + 127, 0) - down, 1)
    scale = np.exp2(byte - 127.0)
    codes = (blocks / scale).astype(np.float32).astype(dtype).astype(np.float64)
    return np.moveaxis((codes * scale).reshape(v.shape), -1, axis)


WIDE = False


def mx_kscale(k):
    if not WIDE:
        return np.ones(k)
    levels = np.array([10, -10, 5, -5, 0])
    if k % 512:
        return np.exp2(np.random.permutation(np.resize(levels, k // 32))).repeat(32)
    a = np.empty((k // 512, 16))
    for p in range(k // 512):
        a[p, :8] = np.random.permutation(np.resize(levels, 8))
        for g in range(8):
            far = levels[np.abs(levels - a[p, g]) >= 10]
            a[p, g + 8] = far[np.random.randint(len(far))]
    return np.exp2(a.ravel()).repeat(32)


def f64(x):
    return np.asarray(x).astype(np.float64)


def striped(idx):
    return np.tile(idx.reshape(-1, 16).T, (8, 1)).astype(np.uint16)


def unstriped(offs):
    return offs[:16].T.reshape(-1).astype(np.int64)


def striped8(idx):
    return np.concatenate([x.reshape(-1, 16).T for x in idx]).astype(np.uint16)


def runs(offs, k):
    lists = np.stack([offs[16 * r : 16 * r + 16].T.reshape(-1) for r in range(8)]).astype(np.int64)
    return lists[np.arange(k) % 512 // 64]


def pack_weight(w):
    k, n = w.shape
    w = f64(np.asarray(w, np.float32).astype(ml_dtypes.bfloat16)).reshape(k // 32, 32, n)
    amax = np.abs(w).max(1)
    byte = np.clip(np.where(amax > 0, np.frexp(amax)[1] - 1 + 127 - 7, 1), 1, 254)
    scaled = (w * np.exp2(127.0 - byte)[:, None, :]).reshape(k, n).astype(np.float32)
    words = np.ascontiguousarray(scaled.reshape(k // 512, 128, 4, n).transpose(0, 1, 3, 2)).astype(ml_dtypes.float8_e4m3fn).view(np.uint8)
    return words, np.ascontiguousarray(byte.astype(np.uint8).reshape(k // 512, 16, n))


def unpack_weight(words, scales):
    g, p, n, _ = words.shape
    vals = np.ascontiguousarray(words).view(ml_dtypes.float8_e4m3fn).astype(np.float64) * np.repeat(np.exp2(scales.astype(np.float64) - 127.0), 8, axis=1)[..., None]
    return vals.transpose(0, 1, 3, 2).reshape(g * 512, n)


def relu(v):
    return np.maximum(v, 0.0)


K, T, S, V, N, H = 512, 2048, 512, 256, 512, 512


def setup_inputs():
    n = np.random.standard_normal
    s = mx_kscale(K)[:, None]
    u = mx_kscale(H)
    packed_xT = pack_weight(n((K, T)) * s)
    perm = np.stack([np.random.permutation(S) for _ in range(8)])
    return {
        "x_words": packed_xT[0],
        "x_scales": packed_xT[1],
        "w1": (n((K, H)) / np.sqrt(K) / s * u).astype(np.float32),
        "w2": (n((H, H)) / np.sqrt(H) / u[:, None] * u).astype(np.float32),
        "w3": (n((H, N)) / np.sqrt(H) / u[:, None]).astype(np.float32),
        "offs": striped(np.random.permutation(T)[:S]),
        "la": striped8(perm[:, :V]),
        "lb": striped8(perm[:, V:]),
    }


def reference(x_words, x_scales, w1, w2, w3, offs, la, lb):
    xq = unpack_weight(x_words, x_scales)[:, unstriped(offs)]
    y = mxq(f64(w1), 0, "e4m3").T @ xq
    z = y[np.arange(H)[:, None], runs(la, H)]
    h = relu(mxq(f64(w2), 0, "e4m3").T @ mxq(z, 0, "e4m3"))
    o = y[np.arange(H)[:, None], runs(lb, H)] - (0.5 * h)
    p = np.zeros((H, S))
    p[np.arange(H)[:, None], runs(la, H)] = h
    z2 = p.copy()
    z2[np.arange(H)[:, None], runs(lb, H)] = o
    return mxq(f64(w3), 0, "e4m3").T @ mxq(z2, 0, "e4m3")

@@ -1,0 +1,209 @@
+from contextlib import ExitStack
+
+import concourse.mybir as mybir
+
+K, T, S, V, N, H = 512, 2048, 512, 256, 512, 512
+FLOPS = 2 * K * H * S + 2 * H * H * V + 2 * H * N * S
+
+F32 = mybir.dt.float32
+BF16 = mybir.dt.bfloat16
+I32 = mybir.dt.int32
+U32 = mybir.dt.uint32
+U16 = mybir.dt.uint16
+U8 = mybir.dt.uint8
+FP8X4 = mybir.dt.float8_e4m3fn_x4
+ACT = mybir.ActivationFunctionType
+ADD = mybir.AluOpType.add
+
+P = 128
+PACK = 4
+HALF = 256
+ORDER = (1, 3, 0, 2)
+
+
+def tile_picked_prunefill_relu_p_kernel(
+    tc, x_words, x_scales, w1, w2, w3, offs, la, lb, out
+):
+    nc = tc.nc
+    with ExitStack() as ctx:
+        keep = ctx.enter_context(tc.tile_pool(name="keep", bufs=1))
+        psum = ctx.enter_context(tc.psum_pool(name="psum", bufs=1))
+
+        def sb(name, shape, dtype, tag=None):
+            return keep.tile(shape, dtype, name=name, tag=tag or name, align_bytes=64)
+
+        def bank(name, b):
+            return psum.tile([P, 512], F32, name=name, tag="bank%d" % b)
+
+        def rows4(w):
+            return w.rearrange("(p j) n -> p j n", j=PACK)
+
+        def quantize(codes, scales, grouped):
+            nc.vector.quantize_mx(out=codes.bitcast(FP8X4), scales=scales, in_=grouped)
+
+        def mm(dst, wc, ws, xc, xsc):
+            nc.tensor.matmul_mx(
+                out=dst, lhsT=wc.bitcast(FP8X4), lhsT_scale=ws,
+                rhs=xc.bitcast(FP8X4), rhs_scale=xsc, start=True, stop=True,
+            )
+
+        offs_t = keep.tile([P, S // 16], U16, name="offs_t")
+        la_t = keep.tile([P, V // 16], U16, name="la_t")
+        lb_t = keep.tile([P, V // 16], U16, name="lb_t")
+        w1_raw = [sb("w1_raw%d" % h, [P, PACK, HALF], F32) for h in range(2)]
+        xw = sb("xw", [P, T], U32)
+        xs = sb("xs", [P, T], U8)
+        w2_raw = [sb("w2_raw%d" % h, [P, PACK, HALF], F32) for h in range(2)]
+        w3_raw = sb("w3_raw", [P, PACK, N], F32)
+
+        nc.vector.memset(xs[:].bitcast(I32), 0)
+        nc.sync.dma_start(offs_t[:], offs)
+        nc.sync.dma_start(w1_raw[0][:], rows4(w1)[:, :, 0:HALF])
+        nc.sync.dma_start(la_t[:], la)
+        nc.sync.dma_start(w1_raw[1][:], rows4(w1)[:, :, HALF:H])
+        for q in range(4):
+            nc.sync.dma_start(
+                xs[32 * q : 32 * q + 4, :].bitcast(I32), x_scales[0, 4 * q : 4 * q + 4, :].bitcast(I32)
+            )
+        nc.sync.dma_start(xw[:].bitcast(I32), x_words[0].rearrange("p n t -> p (n t)").bitcast(I32))
+        nc.sync.dma_start(w2_raw[0][:], rows4(w2)[:, :, 0:HALF])
+        nc.sync.dma_start(w2_raw[1][:], rows4(w2)[:, :, HALF:H])
+        nc.sync.dma_start(w3_raw[:], rows4(w3))
+        nc.sync.dma_start(lb_t[:], lb)
+
+        xg_s = sb("xg_s", [P, S], U8)
+        nc.vector.tensor_copy(xg_s[:], xs[:].indirect(offs_t[:]))
+
+        w1_g = sb("w1_g", [P, PACK * H], BF16)
+        w1_dst = w1_g[:].rearrange("p (t m j) -> p m j t", t=PACK, j=PACK)
+        nc.vector.tensor_copy(w1_dst[:, 0:64], w1_raw[0][:].rearrange("p j (m t) -> p m j t", t=PACK))
+        nc.scalar.copy(w1_dst[:, 64:P], w1_raw[1][:].rearrange("p j (m t) -> p m j t", t=PACK))
+        w1_c = sb("w1_c", [P, H], U32)
+        w1_s = sb("w1_s", [P, H], U8)
+        quantize(w1_c[:], w1_s[:], w1_g[:])
+
+        xg_w = sb("xg_w", [P, S], U32)
+        for h in range(2):
+            nc.vector.tensor_copy(
+                xg_w[:, h * HALF : (h + 1) * HALF], xw[:].indirect(offs_t[:, 16 * h : 16 * h + 16])
+            )
+
+        y = [sb("y%d" % t, [P, S], F32) for t in range(PACK)]
+        halves = [(t, h) for h in range(2) for t in ORDER[:2]]
+        for b, (t, h) in enumerate(halves):
+            acc = bank("y_acc%d" % b, b)
+            cols = slice(h * HALF, (h + 1) * HALF)
+            m = slice(t * P, (t + 1) * P)
+            mm(acc[:, 0:HALF], w1_c[:, m], w1_s[:, m], xg_w[:, cols], xg_s[:, cols])
+            nc.scalar.copy(y[t][:, cols], acc[:, 0:HALF])
+        for b, t in enumerate(ORDER[2:]):
+            acc = bank("y_acc%d" % (4 + b), 4 + b)
+            m = slice(t * P, (t + 1) * P)
+            mm(acc[:], w1_c[:, m], w1_s[:, m], xg_w[:], xg_s[:])
+            nc.scalar.copy(y[t][:], acc[:])
+
+        w2_g = sb("w2_g", [P, PACK * H], BF16)
+        w2_dst = w2_g[:].rearrange("p (t m j) -> p m j t", t=PACK, j=PACK)
+        nc.vector.tensor_copy(w2_dst[:, 0:64], w2_raw[0][:].rearrange("p j (m t) -> p m j t", t=PACK))
+        z_planes = sb("z_planes", [P, PACK, V], BF16)
+        for t in ORDER:
+            nc.vector.tensor_copy(z_planes[:, t, :], y[t][:].indirect(la_t[:]))
+        nc.scalar.copy(w2_dst[:, 64:P], w2_raw[1][:].rearrange("p j (m t) -> p m j t", t=PACK))
+        z_g = sb("z_g", [P, PACK * V], BF16, tag="z_g")
+        nc.scalar.copy(
+            z_g[:].rearrange("p (c i t) -> p c t i", i=4, t=PACK),
+            z_planes[:].rearrange("p t (c i) -> p c t i", i=4),
+        )
+        z_c = sb("z_c", [P, V], U32)
+        z_s = sb("z_s", [P, V], U8)
+        quantize(z_c[:], z_s[:], z_g[:])
+        w2_c = sb("w2_c", [P, H], U32, tag="chain")
+        w2_s = sb("w2_s", [P, H], U8)
+        quantize(w2_c[:], w2_s[:], w2_g[:])
+
+        hh = [sb("h%d" % t, [P, V], F32) for t in range(PACK)]
+        hn = [sb("hn%d" % t, [P, V], F32) for t in range(PACK)]
+        for b, t in enumerate(ORDER):
+            acc = bank("h_acc%d" % t, (6 + b) % 8)
+            m = slice(t * P, (t + 1) * P)
+            mm(acc[:, 0:V], w2_c[:, m], w2_s[:, m], z_c[:], z_s[:])
+            nc.scalar.activation(hh[t][:], acc[:, 0:V], ACT.Relu)
+            nc.scalar.activation(hn[t][:], hh[t][:], ACT.Copy, scale=-0.5)
+
+        lone = {t: sb("z2_%d" % t, [P, S], F32) for t in ORDER[:2]}
+        pair = {t: sb("z2_%d" % t, [P, 2 * S], F32) for t in ORDER[2:]}
+        yb = {}
+
+        def fetch_partner(t, tag):
+            yb[t] = sb("yb%d" % t, [P, V], F32, tag=tag)
+            nc.vector.tensor_copy(yb[t][:], y[t][:].indirect(lb_t[:]))
+
+        def scatter_h(t, window):
+            nc.vector.tensor_copy(window[:].indirect(la_t[:]), hh[t][:])
+
+        def scatter_o(t, window):
+            nc.vector.tensor_tensor(window[:].indirect(lb_t[:]), yb[t][:], hn[t][:], ADD)
+
+        fetch_partner(1, None)
+        fetch_partner(3, None)
+        fetch_partner(0, "z_g")
+        for t in ORDER[:2]:
+            scatter_h(t, lone[t])
+            scatter_o(t, lone[t])
+            nc.scalar.copy(pair[t - 1][:, S : 2 * S], lone[t][:])
+
+        w3_g = sb("w3_g", [P, PACK * N], BF16, tag="chain")
+        nc.scalar.copy(
+            w3_g[:].rearrange("p (c i j) -> p c j i", i=4, j=PACK),
+            w3_raw[:].rearrange("p j (c i) -> p c j i", i=4),
+        )
+        w3_c = sb("w3_c", [P, N], U32)
+        w3_s = sb("w3_s", [P, N], U8)
+        quantize(w3_c[:], w3_s[:], w3_g[:])
+        fetch_partner(2, "chain")
+
+        chunks = [slice(0, 128), slice(128, 256), slice(256, 512)]
+        width = [c.stop - c.start for c in chunks]
+        z2_g = [sb("z2_g%d" % c, [P, width[c], PACK], BF16) for c in range(3)]
+
+        def pair_view(t, c):
+            return pair[t][:].rearrange("p (u c) -> p c u", u=2)[:, chunks[c], :]
+
+        scatter_h(0, pair[0])
+        scatter_o(0, pair[0])
+        for c in range(3):
+            nc.scalar.copy(z2_g[c][:, :, 0:2], pair_view(0, c))
+        scatter_h(2, pair[2])
+        scatter_o(2, pair[2])
+
+        z2_c = [sb("z2_c%d" % c, [P, width[c]], U32) for c in range(3)]
+        z2_s = [sb("z2_s%d" % c, [P, width[c]], U8) for c in range(3)]
+        for c in range(2):
+            nc.vector.tensor_copy(z2_g[c][:, :, 2:4], pair_view(2, c))
+        nc.scalar.copy(z2_g[2][:, :, 2:4], pair_view(2, 2))
+        for c in range(3):
+            quantize(z2_c[c][:], z2_s[c][:], z2_g[c][:].rearrange("p c t -> p (c t)"))
+
+        out_rows = out.rearrange("(t p) n -> p t n", p=P)
+        for c in range(2):
+            acc = bank("o_acc%d" % c, 2 + c)
+            for t in range(PACK):
+                m = slice(t * P, (t + 1) * P)
+                mm(acc[:, m], w3_c[:, m], w3_s[:, m], z2_c[c][:], z2_s[c][:])
+            res = sb("res%d" % c, [P, PACK, P], F32)
+            src = acc[:].rearrange("p (t c) -> p t c", t=PACK)
+            if c == 0:
+                nc.scalar.copy(res[:], src)
+            else:
+                nc.vector.tensor_copy(res[:], src)
+            nc.sync.dma_start(out_rows[:, :, chunks[c]], res[:])
+        for t in range(PACK):
+            acc = bank("o_acc2%d" % t, 4 + t)
+            m = slice(t * P, (t + 1) * P)
+            mm(acc[:, 0:HALF], w3_c[:, m], w3_s[:, m], z2_c[2][:], z2_s[2][:])
+            res = sb("res2%d" % t, [P, HALF], F32)
+            if t % 2 == 0:
+                nc.scalar.copy(res[:], acc[:, 0:HALF])
+            else:
+                nc.vector.tensor_copy(res[:], acc[:, 0:HALF])
+            nc.sync.dma_start(out_rows[:, t, chunks[2]], res[:])

@@ -50,17 +50,17 @@ def tile_picked_prunefill_relu_p_kernel(
         offs_t = keep.tile([P, S // 16], U16, name="offs_t")
         la_t = keep.tile([P, V // 16], U16, name="la_t")
         lb_t = keep.tile([P, V // 16], U16, name="lb_t")
-        w1_raw = [sb("w1_raw%d" % h, [P, PACK, HALF], F32) for h in range(2)]
+        w1_raw = sb("w1_raw", [P, PACK, H], F32)
         xw = sb("xw", [P, T], U32)
-        xs = sb("xs", [P, T], U8)
+        xs = sb("xs", [P, T], U8, tag="xs_w1c")
         w2_raw = [sb("w2_raw%d" % h, [P, PACK, HALF], F32) for h in range(2)]
         w3_raw = sb("w3_raw", [P, PACK, N], F32)
 
         nc.vector.memset(xs[:].bitcast(I32), 0)
         nc.sync.dma_start(offs_t[:], offs)
-        nc.sync.dma_start(w1_raw[0][:], rows4(w1)[:, :, 0:HALF])
+        nc.sync.dma_start(w1_raw[:], rows4(w1))
         nc.sync.dma_start(la_t[:], la)
-        nc.sync.dma_start(w1_raw[1][:], rows4(w1)[:, :, HALF:H])
+        nc.sync.dma_start(lb_t[:], lb)
         for q in range(4):
             nc.sync.dma_start(
                 xs[32 * q : 32 * q + 4, :].bitcast(I32), x_scales[0, 4 * q : 4 * q + 4, :].bitcast(I32)
@@ -69,46 +69,46 @@ def tile_picked_prunefill_relu_p_kernel(
         nc.sync.dma_start(w2_raw[0][:], rows4(w2)[:, :, 0:HALF])
         nc.sync.dma_start(w2_raw[1][:], rows4(w2)[:, :, HALF:H])
         nc.sync.dma_start(w3_raw[:], rows4(w3))
-        nc.sync.dma_start(lb_t[:], lb)
 
         xg_s = sb("xg_s", [P, S], U8)
         nc.vector.tensor_copy(xg_s[:], xs[:].indirect(offs_t[:]))
 
-        w1_g = sb("w1_g", [P, PACK * H], BF16)
-        w1_dst = w1_g[:].rearrange("p (t m j) -> p m j t", t=PACK, j=PACK)
-        nc.vector.tensor_copy(w1_dst[:, 0:64], w1_raw[0][:].rearrange("p j (m t) -> p m j t", t=PACK))
-        nc.scalar.copy(w1_dst[:, 64:P], w1_raw[1][:].rearrange("p j (m t) -> p m j t", t=PACK))
-        w1_c = sb("w1_c", [P, H], U32)
+        w1_g = sb("w1_g", [P, PACK * H], BF16, tag="w1g_xg")
+        w1_dst = w1_g[:].rearrange("p (t m j) -> p m t j", t=PACK, j=PACK)
+        w1_src = w1_raw[:].rearrange("p j (m t) -> p m t j", t=PACK)
+        nc.vector.tensor_copy(w1_dst[:, 0:48], w1_src[:, 0:48])
+        nc.scalar.copy(w1_dst[:, 48:P], w1_src[:, 48:P])
+        w1_c = sb("w1_c", [P, H], U32, tag="xs_w1c")
         w1_s = sb("w1_s", [P, H], U8)
         quantize(w1_c[:], w1_s[:], w1_g[:])
 
-        xg_w = sb("xg_w", [P, S], U32)
+        xg_w = [sb("xg_w%d" % h, [P, HALF], U32, tag=("w1g_xg", "w1_raw")[h])[:] for h in range(2)]
         for h in range(2):
-            nc.vector.tensor_copy(
-                xg_w[:, h * HALF : (h + 1) * HALF], xw[:].indirect(offs_t[:, 16 * h : 16 * h + 16])
-            )
+            nc.vector.tensor_copy(xg_w[h], xw[:].indirect(offs_t[:, 16 * h : 16 * h + 16]))
 
-        y = [sb("y%d" % t, [P, S], F32) for t in range(PACK)]
+        y = [sb("y%d" % t, [P, S + V if t == 2 else S], F32) for t in range(PACK)]
         halves = [(t, h) for h in range(2) for t in ORDER[:2]]
         for b, (t, h) in enumerate(halves):
             acc = bank("y_acc%d" % b, b)
             cols = slice(h * HALF, (h + 1) * HALF)
             m = slice(t * P, (t + 1) * P)
-            mm(acc[:, 0:HALF], w1_c[:, m], w1_s[:, m], xg_w[:, cols], xg_s[:, cols])
+            mm(acc[:, 0:HALF], w1_c[:, m], w1_s[:, m], xg_w[h], xg_s[:, cols])
             nc.scalar.copy(y[t][:, cols], acc[:, 0:HALF])
         for b, t in enumerate(ORDER[2:]):
             acc = bank("y_acc%d" % (4 + b), 4 + b)
             m = slice(t * P, (t + 1) * P)
-            mm(acc[:], w1_c[:, m], w1_s[:, m], xg_w[:], xg_s[:])
-            nc.scalar.copy(y[t][:], acc[:])
+            for h in range(2):
+                cols = slice(h * HALF, (h + 1) * HALF)
+                mm(acc[:, cols], w1_c[:, m], w1_s[:, m], xg_w[h], xg_s[:, cols])
+            nc.scalar.copy(y[t][:, 0:S], acc[:])
 
         w2_g = sb("w2_g", [P, PACK * H], BF16)
-        w2_dst = w2_g[:].rearrange("p (t m j) -> p m j t", t=PACK, j=PACK)
-        nc.vector.tensor_copy(w2_dst[:, 0:64], w2_raw[0][:].rearrange("p j (m t) -> p m j t", t=PACK))
+        w2_dst = w2_g[:].rearrange("p (t m j) -> p m t j", t=PACK, j=PACK)
+        nc.vector.tensor_copy(w2_dst[:, 0:64], w2_raw[0][:].rearrange("p j (m t) -> p m t j", t=PACK))
         z_planes = sb("z_planes", [P, PACK, V], BF16)
         for t in ORDER:
             nc.vector.tensor_copy(z_planes[:, t, :], y[t][:].indirect(la_t[:]))
-        nc.scalar.copy(w2_dst[:, 64:P], w2_raw[1][:].rearrange("p j (m t) -> p m j t", t=PACK))
+        nc.scalar.copy(w2_dst[:, 64:P], w2_raw[1][:].rearrange("p j (m t) -> p m t j", t=PACK))
         z_g = sb("z_g", [P, PACK * V], BF16, tag="z_g")
         nc.scalar.copy(
             z_g[:].rearrange("p (c i t) -> p c t i", i=4, t=PACK),
@@ -123,34 +123,54 @@ def tile_picked_prunefill_relu_p_kernel(
 
         hh = [sb("h%d" % t, [P, V], F32) for t in range(PACK)]
         hn = [sb("hn%d" % t, [P, V], F32) for t in range(PACK)]
+        h_acc = {}
         for b, t in enumerate(ORDER):
-            acc = bank("h_acc%d" % t, (6 + b) % 8)
+            h_acc[t] = bank("h_acc%d" % t, (6 + b) % 8)
             m = slice(t * P, (t + 1) * P)
-            mm(acc[:, 0:V], w2_c[:, m], w2_s[:, m], z_c[:], z_s[:])
-            nc.scalar.activation(hh[t][:], acc[:, 0:V], ACT.Relu)
+            mm(h_acc[t][:, 0:V], w2_c[:, m], w2_s[:, m], z_c[:], z_s[:])
+
+        def relu(t):
+            nc.scalar.activation(hh[t][:], h_acc[t][:, 0:V], ACT.Relu)
+
+        def negative_half(t):
             nc.scalar.activation(hn[t][:], hh[t][:], ACT.Copy, scale=-0.5)
+
+        for t in ORDER[:2]:
+            relu(t)
+        for t in ORDER[:2]:
+            negative_half(t)
+        for t in ORDER[2:]:
+            relu(t)
 
         lone = {t: sb("z2_%d" % t, [P, S], F32) for t in ORDER[:2]}
         pair = {t: sb("z2_%d" % t, [P, 2 * S], F32) for t in ORDER[2:]}
         yb = {}
 
-        def fetch_partner(t, tag):
-            yb[t] = sb("yb%d" % t, [P, V], F32, tag=tag)
-            nc.vector.tensor_copy(yb[t][:], y[t][:].indirect(lb_t[:]))
+        def fetch_partner(t, dst):
+            yb[t] = dst
+            nc.vector.tensor_copy(dst, y[t][:].indirect(lb_t[:]))
 
         def scatter_h(t, window):
             nc.vector.tensor_copy(window[:].indirect(la_t[:]), hh[t][:])
 
         def scatter_o(t, window):
-            nc.vector.tensor_tensor(window[:].indirect(lb_t[:]), yb[t][:], hn[t][:], ADD)
+            nc.vector.tensor_tensor(window[:].indirect(lb_t[:]), yb[t], hn[t][:], ADD)
 
-        fetch_partner(1, None)
-        fetch_partner(3, None)
-        fetch_partner(0, "z_g")
+        fetch_partner(1, y[2][:, S : S + V])
+        yb_late = sb("yb_late", [P, 2 * V], F32, tag="z_g")
+        fetch_partner(3, yb_late[:, 0:V])
+        fetch_partner(0, yb_late[:, V : 2 * V])
         for t in ORDER[:2]:
             scatter_h(t, lone[t])
+        for t in ORDER[:2]:
             scatter_o(t, lone[t])
+        for t in ORDER[:2]:
             nc.scalar.copy(pair[t - 1][:, S : 2 * S], lone[t][:])
+        for t in ORDER[2:]:
+            negative_half(t)
+        for t in ORDER[2:]:
+            scatter_h(t, pair[t])
+        scatter_o(0, pair[0])
 
         w3_g = sb("w3_g", [P, PACK * N], BF16, tag="chain")
         nc.scalar.copy(
@@ -160,7 +180,7 @@ def tile_picked_prunefill_relu_p_kernel(
         w3_c = sb("w3_c", [P, N], U32)
         w3_s = sb("w3_s", [P, N], U8)
         quantize(w3_c[:], w3_s[:], w3_g[:])
-        fetch_partner(2, "chain")
+        fetch_partner(2, sb("yb2", [P, V], F32, tag="chain")[:])
 
         chunks = [slice(0, 128), slice(128, 256), slice(256, 512)]
         width = [c.stop - c.start for c in chunks]
@@ -169,11 +189,8 @@ def tile_picked_prunefill_relu_p_kernel(
         def pair_view(t, c):
             return pair[t][:].rearrange("p (u c) -> p c u", u=2)[:, chunks[c], :]
 
-        scatter_h(0, pair[0])
-        scatter_o(0, pair[0])
         for c in range(3):
             nc.scalar.copy(z2_g[c][:, :, 0:2], pair_view(0, c))
-        scatter_h(2, pair[2])
         scatter_o(2, pair[2])
 
         z2_c = [sb("z2_c%d" % c, [P, width[c]], U32) for c in range(3)]
@@ -185,25 +202,22 @@ def tile_picked_prunefill_relu_p_kernel(
             quantize(z2_c[c][:], z2_s[c][:], z2_g[c][:].rearrange("p c t -> p (c t)"))
 
         out_rows = out.rearrange("(t p) n -> p t n", p=P)
-        for c in range(2):
-            acc = bank("o_acc%d" % c, 2 + c)
-            for t in range(PACK):
-                m = slice(t * P, (t + 1) * P)
-                mm(acc[:, m], w3_c[:, m], w3_s[:, m], z2_c[c][:], z2_s[c][:])
-            res = sb("res%d" % c, [P, PACK, P], F32)
-            src = acc[:].rearrange("p (t c) -> p t c", t=PACK)
-            if c == 0:
-                nc.scalar.copy(res[:], src)
-            else:
-                nc.vector.tensor_copy(res[:], src)
-            nc.sync.dma_start(out_rows[:, :, chunks[c]], res[:])
+        for u in range(2):
+            acc = bank("o_acc0%d" % u, u)
+            for e in range(2):
+                m = slice((2 * u + e) * P, (2 * u + e + 1) * P)
+                mm(acc[:, e * P : (e + 1) * P], w3_c[:, m], w3_s[:, m], z2_c[0][:], z2_s[0][:])
+            res = sb("res0%d" % u, [P, 2, P], F32)
+            nc.scalar.copy(res[:], acc[:, 0 : 2 * P].rearrange("p (t c) -> p t c", t=2))
+            nc.sync.dma_start(out_rows[:, 2 * u : 2 * u + 2, chunks[0]], res[:])
         for t in range(PACK):
-            acc = bank("o_acc2%d" % t, 4 + t)
+            acc = bank("o_acc1%d" % t, 2 + t)
             m = slice(t * P, (t + 1) * P)
-            mm(acc[:, 0:HALF], w3_c[:, m], w3_s[:, m], z2_c[2][:], z2_s[2][:])
-            res = sb("res2%d" % t, [P, HALF], F32)
+            for c in (1, 2):
+                mm(acc[:, chunks[c]], w3_c[:, m], w3_s[:, m], z2_c[c][:], z2_s[c][:])
+            res = sb("res1%d" % t, [P, S - P], F32)
             if t % 2 == 0:
-                nc.scalar.copy(res[:], acc[:, 0:HALF])
+                nc.vector.tensor_copy(res[:], acc[:, P:S])
             else:
-                nc.vector.tensor_copy(res[:], acc[:, 0:HALF])
-            nc.sync.dma_start(out_rows[:, t, chunks[2]], res[:])
+                nc.scalar.copy(res[:], acc[:, P:S])
+            nc.sync.dma_start(out_rows[:, t, P:S], res[:])

from contextlib import ExitStack

import concourse.mybir as mybir

K, T, S, V, N, H = 512, 2048, 512, 256, 512, 512
FLOPS = 2 * K * H * S + 2 * H * H * V + 2 * H * N * S

F32 = mybir.dt.float32
BF16 = mybir.dt.bfloat16
I32 = mybir.dt.int32
U32 = mybir.dt.uint32
U16 = mybir.dt.uint16
U8 = mybir.dt.uint8
FP8X4 = mybir.dt.float8_e4m3fn_x4
ACT = mybir.ActivationFunctionType
ADD = mybir.AluOpType.add

P = 128
PACK = 4
HALF = 256
ORDER = (1, 3, 0, 2)


def tile_picked_prunefill_relu_p_kernel(
    tc, x_words, x_scales, w1, w2, w3, offs, la, lb, out
):
    nc = tc.nc
    with ExitStack() as ctx:
        keep = ctx.enter_context(tc.tile_pool(name="keep", bufs=1))
        psum = ctx.enter_context(tc.psum_pool(name="psum", bufs=1))

        def sb(name, shape, dtype, tag=None):
            return keep.tile(shape, dtype, name=name, tag=tag or name, align_bytes=64)

        def bank(name, b):
            return psum.tile([P, 512], F32, name=name, tag="bank%d" % b)

        def rows4(w):
            return w.rearrange("(p j) n -> p j n", j=PACK)

        def quantize(codes, scales, grouped):
            nc.vector.quantize_mx(out=codes.bitcast(FP8X4), scales=scales, in_=grouped)

        def mm(dst, wc, ws, xc, xsc):
            nc.tensor.matmul_mx(
                out=dst, lhsT=wc.bitcast(FP8X4), lhsT_scale=ws,
                rhs=xc.bitcast(FP8X4), rhs_scale=xsc, start=True, stop=True,
            )

        offs_t = keep.tile([P, S // 16], U16, name="offs_t")
        la_t = keep.tile([P, V // 16], U16, name="la_t")
        lb_t = keep.tile([P, V // 16], U16, name="lb_t")
        w1_raw = sb("w1_raw", [P, PACK, H], F32)
        xw = sb("xw", [P, T], U32)
        xs = sb("xs", [P, T], U8, tag="xs_w1c")
        w2_raw = [sb("w2_raw%d" % h, [P, PACK, HALF], F32) for h in range(2)]
        w3_raw = sb("w3_raw", [P, PACK, N], F32)

        nc.vector.memset(xs[:].bitcast(I32), 0)
        nc.sync.dma_start(offs_t[:], offs)
        nc.sync.dma_start(w1_raw[:], rows4(w1))
        nc.sync.dma_start(la_t[:], la)
        nc.sync.dma_start(lb_t[:], lb)
        for q in range(4):
            nc.sync.dma_start(
                xs[32 * q : 32 * q + 4, :].bitcast(I32), x_scales[0, 4 * q : 4 * q + 4, :].bitcast(I32)
            )
        nc.sync.dma_start(xw[:].bitcast(I32), x_words[0].rearrange("p n t -> p (n t)").bitcast(I32))
        nc.sync.dma_start(w2_raw[0][:], rows4(w2)[:, :, 0:HALF])
        nc.sync.dma_start(w2_raw[1][:], rows4(w2)[:, :, HALF:H])
        nc.sync.dma_start(w3_raw[:], rows4(w3))

        xg_s = sb("xg_s", [P, S], U8)
        nc.vector.tensor_copy(xg_s[:], xs[:].indirect(offs_t[:]))

        w1_g = sb("w1_g", [P, PACK * H], BF16, tag="w1g_xg")
        w1_dst = w1_g[:].rearrange("p (t m j) -> p m t j", t=PACK, j=PACK)
        w1_src = w1_raw[:].rearrange("p j (m t) -> p m t j", t=PACK)
        nc.vector.tensor_copy(w1_dst[:, 0:48], w1_src[:, 0:48])
        nc.scalar.copy(w1_dst[:, 48:P], w1_src[:, 48:P])
        w1_c = sb("w1_c", [P, H], U32, tag="xs_w1c")
        w1_s = sb("w1_s", [P, H], U8)
        quantize(w1_c[:], w1_s[:], w1_g[:])

        xg_w = [sb("xg_w%d" % h, [P, HALF], U32, tag=("w1g_xg", "w1_raw")[h])[:] for h in range(2)]
        for h in range(2):
            nc.vector.tensor_copy(xg_w[h], xw[:].indirect(offs_t[:, 16 * h : 16 * h + 16]))

        y = [sb("y%d" % t, [P, S + V if t == 2 else S], F32) for t in range(PACK)]
        halves = [(t, h) for h in range(2) for t in ORDER[:2]]
        for b, (t, h) in enumerate(halves):
            acc = bank("y_acc%d" % b, b)
            cols = slice(h * HALF, (h + 1) * HALF)
            m = slice(t * P, (t + 1) * P)
            mm(acc[:, 0:HALF], w1_c[:, m], w1_s[:, m], xg_w[h], xg_s[:, cols])
            nc.scalar.copy(y[t][:, cols], acc[:, 0:HALF])
        for b, t in enumerate(ORDER[2:]):
            acc = bank("y_acc%d" % (4 + b), 4 + b)
            m = slice(t * P, (t + 1) * P)
            for h in range(2):
                cols = slice(h * HALF, (h + 1) * HALF)
                mm(acc[:, cols], w1_c[:, m], w1_s[:, m], xg_w[h], xg_s[:, cols])
            nc.scalar.copy(y[t][:, 0:S], acc[:])

        w2_g = sb("w2_g", [P, PACK * H], BF16)
        w2_dst = w2_g[:].rearrange("p (t m j) -> p m t j", t=PACK, j=PACK)
        nc.vector.tensor_copy(w2_dst[:, 0:64], w2_raw[0][:].rearrange("p j (m t) -> p m t j", t=PACK))
        z_planes = sb("z_planes", [P, PACK, V], BF16)
        for t in ORDER:
            nc.vector.tensor_copy(z_planes[:, t, :], y[t][:].indirect(la_t[:]))
        nc.scalar.copy(w2_dst[:, 64:P], w2_raw[1][:].rearrange("p j (m t) -> p m t j", t=PACK))
        z_g = sb("z_g", [P, PACK * V], BF16, tag="z_g")
        nc.scalar.copy(
            z_g[:].rearrange("p (c i t) -> p c t i", i=4, t=PACK),
            z_planes[:].rearrange("p t (c i) -> p c t i", i=4),
        )
        z_c = sb("z_c", [P, V], U32)
        z_s = sb("z_s", [P, V], U8)
        quantize(z_c[:], z_s[:], z_g[:])
        w2_c = sb("w2_c", [P, H], U32, tag="chain")
        w2_s = sb("w2_s", [P, H], U8)
        quantize(w2_c[:], w2_s[:], w2_g[:])

        hh = [sb("h%d" % t, [P, V], F32) for t in range(PACK)]
        hn = [sb("hn%d" % t, [P, V], F32) for t in range(PACK)]
        h_acc = {}
        for b, t in enumerate(ORDER):
            h_acc[t] = bank("h_acc%d" % t, (6 + b) % 8)
            m = slice(t * P, (t + 1) * P)
            mm(h_acc[t][:, 0:V], w2_c[:, m], w2_s[:, m], z_c[:], z_s[:])

        def relu(t):
            nc.scalar.activation(hh[t][:], h_acc[t][:, 0:V], ACT.Relu)

        def negative_half(t):
            nc.scalar.activation(hn[t][:], hh[t][:], ACT.Copy, scale=-0.5)

        for t in ORDER[:2]:
            relu(t)
        for t in ORDER[:2]:
            negative_half(t)
        for t in ORDER[2:]:
            relu(t)

        lone = {t: sb("z2_%d" % t, [P, S], F32) for t in ORDER[:2]}
        pair = {t: sb("z2_%d" % t, [P, 2 * S], F32) for t in ORDER[2:]}
        yb = {}

        def fetch_partner(t, dst):
            yb[t] = dst
            nc.vector.tensor_copy(dst, y[t][:].indirect(lb_t[:]))

        def scatter_h(t, window):
            nc.vector.tensor_copy(window[:].indirect(la_t[:]), hh[t][:])

        def scatter_o(t, window):
            nc.vector.tensor_tensor(window[:].indirect(lb_t[:]), yb[t], hn[t][:], ADD)

        fetch_partner(1, y[2][:, S : S + V])
        yb_late = sb("yb_late", [P, 2 * V], F32, tag="z_g")
        fetch_partner(3, yb_late[:, 0:V])
        fetch_partner(0, yb_late[:, V : 2 * V])
        for t in ORDER[:2]:
            scatter_h(t, lone[t])
        for t in ORDER[:2]:
            scatter_o(t, lone[t])
        for t in ORDER[:2]:
            nc.scalar.copy(pair[t - 1][:, S : 2 * S], lone[t][:])
        for t in ORDER[2:]:
            negative_half(t)
        for t in ORDER[2:]:
            scatter_h(t, pair[t])
        scatter_o(0, pair[0])

        w3_g = sb("w3_g", [P, PACK * N], BF16, tag="chain")
        nc.scalar.copy(
            w3_g[:].rearrange("p (c i j) -> p c j i", i=4, j=PACK),
            w3_raw[:].rearrange("p j (c i) -> p c j i", i=4),
        )
        w3_c = sb("w3_c", [P, N], U32)
        w3_s = sb("w3_s", [P, N], U8)
        quantize(w3_c[:], w3_s[:], w3_g[:])
        fetch_partner(2, sb("yb2", [P, V], F32, tag="chain")[:])

        chunks = [slice(0, 128), slice(128, 256), slice(256, 512)]
        width = [c.stop - c.start for c in chunks]
        z2_g = [sb("z2_g%d" % c, [P, width[c], PACK], BF16) for c in range(3)]

        def pair_view(t, c):
            return pair[t][:].rearrange("p (u c) -> p c u", u=2)[:, chunks[c], :]

        for c in range(3):
            nc.scalar.copy(z2_g[c][:, :, 0:2], pair_view(0, c))
        scatter_o(2, pair[2])

        z2_c = [sb("z2_c%d" % c, [P, width[c]], U32) for c in range(3)]
        z2_s = [sb("z2_s%d" % c, [P, width[c]], U8) for c in range(3)]
        for c in range(2):
            nc.vector.tensor_copy(z2_g[c][:, :, 2:4], pair_view(2, c))
        nc.scalar.copy(z2_g[2][:, :, 2:4], pair_view(2, 2))
        for c in range(3):
            quantize(z2_c[c][:], z2_s[c][:], z2_g[c][:].rearrange("p c t -> p (c t)"))

        out_rows = out.rearrange("(t p) n -> p t n", p=P)
        for u in range(2):
            acc = bank("o_acc0%d" % u, u)
            for e in range(2):
                m = slice((2 * u + e) * P, (2 * u + e + 1) * P)
                mm(acc[:, e * P : (e + 1) * P], w3_c[:, m], w3_s[:, m], z2_c[0][:], z2_s[0][:])
            res = sb("res0%d" % u, [P, 2, P], F32)
            nc.scalar.copy(res[:], acc[:, 0 : 2 * P].rearrange("p (t c) -> p t c", t=2))
            nc.sync.dma_start(out_rows[:, 2 * u : 2 * u + 2, chunks[0]], res[:])
        for t in range(PACK):
            acc = bank("o_acc1%d" % t, 2 + t)
            m = slice(t * P, (t + 1) * P)
            for c in (1, 2):
                mm(acc[:, chunks[c]], w3_c[:, m], w3_s[:, m], z2_c[c][:], z2_s[c][:])
            res = sb("res1%d" % t, [P, S - P], F32)
            if t % 2 == 0:
                nc.vector.tensor_copy(res[:], acc[:, P:S])
            else:
                nc.scalar.copy(res[:], acc[:, P:S])
            nc.sync.dma_start(out_rows[:, t, P:S], res[:])
